import numpy as np
import ml_dtypes


def mxq(x, axis, fmt="e4m3"):
    dtype, down = {"e4m3": (ml_dtypes.float8_e4m3fn, 7), "e5m2": (ml_dtypes.float8_e5m2, 14)}[fmt]
    v = np.moveaxis(np.asarray(x, np.float32).astype(ml_dtypes.bfloat16).astype(np.float64), axis, -1)
    blocks = v.reshape(v.shape[:-1] + (-1, 32))
    amax = np.abs(blocks).max(-1, keepdims=True)
    byte = np.maximum(np.where(amax > 0, np.frexp(amax)[1] - 1 + 127, 0) - down, 1)
    scale = np.exp2(byte - 127.0)
    codes = (blocks / scale).astype(np.float32).astype(dtype).astype(np.float64)
    return np.moveaxis((codes * scale).reshape(v.shape), -1, axis)


WIDE = False


def mx_kscale(k):
    if not WIDE:
        return np.ones(k)
    levels = np.array([10, -10, 5, -5, 0])
    if k % 512:
        return np.exp2(np.random.permutation(np.resize(levels, k // 32))).repeat(32)
    a = np.empty((k // 512, 16))
    for p in range(k // 512):
        a[p, :8] = np.random.permutation(np.resize(levels, 8))
        for g in range(8):
            far = levels[np.abs(levels - a[p, g]) >= 10]
            a[p, g + 8] = far[np.random.randint(len(far))]
    return np.exp2(a.ravel()).repeat(32)


def f64(x):
    return np.asarray(x).astype(np.float64)


def striped(idx):
    return np.tile(idx.reshape(-1, 16).T, (8, 1)).astype(np.uint16)


def unstriped(offs):
    return offs[:16].T.reshape(-1).astype(np.int64)


def striped8(idx):
    return np.concatenate([x.reshape(-1, 16).T for x in idx]).astype(np.uint16)


def runs(offs, k):
    lists = np.stack([offs[16 * r : 16 * r + 16].T.reshape(-1) for r in range(8)]).astype(np.int64)
    return lists[np.arange(k) % 512 // 64]


def pack_weight(w):
    k, n = w.shape
    w = f64(np.asarray(w, np.float32).astype(ml_dtypes.bfloat16)).reshape(k // 32, 32, n)
    amax = np.abs(w).max(1)
    byte = np.clip(np.where(amax > 0, np.frexp(amax)[1] - 1 + 127 - 7, 1), 1, 254)
    scaled = (w * np.exp2(127.0 - byte)[:, None, :]).reshape(k, n).astype(np.float32)
    words = np.ascontiguousarray(scaled.reshape(k // 512, 128, 4, n).transpose(0, 1, 3, 2)).astype(ml_dtypes.float8_e4m3fn).view(np.uint8)
    return words, np.ascontiguousarray(byte.astype(np.uint8).reshape(k // 512, 16, n))


def unpack_weight(words, scales):
    g, p, n, _ = words.shape
    vals = np.ascontiguousarray(words).view(ml_dtypes.float8_e4m3fn).astype(np.float64) * np.repeat(np.exp2(scales.astype(np.float64) - 127.0), 8, axis=1)[..., None]
    return vals.transpose(0, 1, 3, 2).reshape(g * 512, n)


K, T, S, V, N, H = 512, 2048, 512, 256, 512, 512


def setup_inputs():
    n = np.random.standard_normal
    s = mx_kscale(K)[:, None]
    u = mx_kscale(S)
    packed_xT = pack_weight(n((K, T)) * s)
    perm = np.stack([np.random.permutation(H) for _ in range(8)])
    return {
        "x_words": packed_xT[0],
        "x_scales": packed_xT[1],
        "wa": (n((K, H)) / np.sqrt(K) / s).astype(np.float32),
        "wb": (n((K, N)) / np.sqrt(K) / s).astype(np.float32),
        "gt": (np.random.uniform(0.5, 1.5, (S, 1)) * u[:, None]).astype(np.float32),
        "gi": (np.random.uniform(0.5, 1.5, (S, 1)) / u[:, None]).astype(np.float32),
        "offs": striped(np.random.permutation(T)[:S]),
        "two": striped(np.random.permutation(T)[:S]),
        "la": striped8(perm[:, :V]),
        "lb": striped8(perm[:, V:]),
    }


def reference(x_words, x_scales, wa, wb, gt, gi, offs, two, la, lb):
    xq = unpack_weight(x_words, x_scales)[:, unstriped(offs)]
    a = xq.T @ mxq(f64(wa), 0, "e4m3")
    p = a[np.arange(S)[:, None], runs(la, S)]
    qv = a[np.arange(S)[:, None], runs(lb, S)]
    lo = np.minimum(p, qv)
    hi = np.maximum(p, qv)
    d1 = np.zeros((S, H))
    d1[np.arange(S)[:, None], runs(la, S)] = hi
    d2 = d1.copy()
    d2[np.arange(S)[:, None], runs(lb, S)] = lo
    z = f64(gt) * d2
    x_two = unpack_weight(x_words, x_scales)[:, unstriped(two)]
    b = x_two.T @ mxq(f64(wb), 0, "e4m3")
    z2 = f64(gi) * b
    cv = 0.0625 * ((mxq(z, 0, "e4m3").T @ mxq(z2, 0, "e4m3")))
    return cv

@@ -1,0 +1,196 @@
+from contextlib import ExitStack
+
+import concourse.mybir as mybir
+
+K, T, S, V, N, H = 512, 2048, 512, 256, 512, 512
+FLOPS = 2 * S * K * H + 2 * S * K * N + 2 * S * H * N
+
+F32 = mybir.dt.float32
+BF16 = mybir.dt.bfloat16
+I32 = mybir.dt.int32
+U32 = mybir.dt.uint32
+U16 = mybir.dt.uint16
+U8 = mybir.dt.uint8
+FP8X4 = mybir.dt.float8_e4m3fn_x4
+ALU = mybir.AluOpType
+COPY = mybir.ActivationFunctionType.Copy
+
+P = 128
+PACK = 4
+LINE = 4
+
+
+def weave(engine_copy, woven, planes, first, last):
+    engine_copy(
+        out=woven[:, first:last, :].rearrange("p (c i) t -> p c t i", i=LINE),
+        in_=planes[:, :, first:last].rearrange("p t (c i) -> p c t i", i=LINE),
+    )
+
+
+def tile_picked_momord_none_p_kernel(
+    tc, x_words, x_scales, wa, wb, gt, gi, offs, two, la, lb, out
+):
+    nc = tc.nc
+
+    with ExitStack() as ctx:
+        keep = ctx.enter_context(tc.tile_pool(name="keep", bufs=1))
+        psum = ctx.enter_context(tc.psum_pool(name="psum", bufs=1))
+
+        def quantize(name, woven, first, last, codes, scales):
+            nc.vector.quantize_mx(
+                out=codes[:, first:last].bitcast(FP8X4),
+                scales=scales[:, first:last],
+                in_=woven[:, first:last, :].rearrange("p c t -> p (c t)"),
+            )
+
+        table_scales = keep.tile([P, T], U8, name="table_scales")
+        nc.gpsimd.memset(table_scales[:].bitcast(I32), 0)
+        offs_sb = keep.tile([P, S // 16], U16, name="offs_sb")
+        nc.sync.dma_start(offs_sb[:], offs)
+        for r in range(4):
+            nc.scalar.dma_start(table_scales[r:P:32, :].bitcast(I32), x_scales[0, r:16:4, :].bitcast(I32))
+        wa_raw = keep.tile([P, PACK, H], F32, name="wa_raw")
+        nc.sync.dma_start(wa_raw[:], wa.rearrange("(p j) c -> p j c", j=PACK))
+        table_words = keep.tile([P, T], U32, name="table_words")
+        nc.sync.dma_start(table_words[:].bitcast(I32), x_words[0].rearrange("p n r -> p (n r)").bitcast(I32))
+        gt_sb = keep.tile([P, PACK], F32, name="gt_sb")
+        nc.sync.dma_start(gt_sb[:], gt.rearrange("(p t) o -> p (t o)", t=PACK))
+        gi_sb = keep.tile([P, PACK], F32, name="gi_sb")
+        nc.sync.dma_start(gi_sb[:], gi.rearrange("(p t) o -> p (t o)", t=PACK))
+        two_sb = keep.tile([P, S // 16], U16, name="two_sb")
+        nc.sync.dma_start(two_sb[:], two)
+        la_sb = keep.tile([P, V // 16], U16, name="la_sb")
+        nc.sync.dma_start(la_sb[:], la)
+        lb_sb = keep.tile([P, V // 16], U16, name="lb_sb")
+        nc.sync.dma_start(lb_sb[:], lb)
+        wb_raw = keep.tile([P, PACK, N], F32, name="wb_raw", tag="wb_raw")
+        nc.sync.dma_start(wb_raw[:], wb.rearrange("(p j) c -> p j c", j=PACK))
+
+        def pick(name, dtype, table, offsets, tag=None):
+            picked = keep.tile([P, S], dtype, name=name, tag=tag or name, align_bytes=64)
+            nc.vector.tensor_copy(picked[:].rearrange("p (t m) -> p m t", t=PACK), table[:].indirect(offsets[:]))
+            return picked
+
+        xa_scales = pick("xa_scales", U8, table_scales, offs_sb)
+        wa_woven = keep.tile([P, H, PACK], BF16, name="wa_woven", tag="wa_woven", align_bytes=64)
+        weave(nc.scalar.copy, wa_woven, wa_raw, 0, 320)
+        weave(nc.vector.tensor_copy, wa_woven, wa_raw, 320, H)
+        gt_abs = keep.tile([P, PACK], F32, name="gt_abs")
+        nc.vector.scalar_tensor_tensor(gt_abs[:], gt_sb[:], -1.0, gt_sb[:], ALU.mult, ALU.max)
+        gt_pos = keep.tile([P, PACK], F32, name="gt_pos")
+        nc.vector.tensor_scalar(gt_pos[:], gt_sb[:], 0.0, 2.0, ALU.is_ge, ALU.mult)
+        wa_codes = keep.tile([P, H], U32, name="wa_codes", align_bytes=64)
+        wa_scales = keep.tile([P, H], U8, name="wa_scales", align_bytes=64)
+        quantize("wa", wa_woven, 0, H, wa_codes, wa_scales)
+        gi_signed = keep.tile([P, PACK], F32, name="gi_signed")
+        nc.vector.scalar_tensor_tensor(gi_signed[:], gt_pos[:], -1.0, gi_sb[:], ALU.add, ALU.mult)
+        xa_words = pick("xa_words", U32, table_words, offs_sb)
+
+        def product(tag, words, scales, m0, codes, code_scales):
+            bank = psum.tile([P, 512], F32, name=tag, tag=tag)
+            nc.tensor.matmul_mx(
+                out=bank[:],
+                lhsT=words[:, m0 : m0 + P].bitcast(FP8X4),
+                lhsT_scale=scales[:, m0 : m0 + P],
+                rhs=codes[:].bitcast(FP8X4),
+                rhs_scale=code_scales[:],
+                start=True,
+                stop=True,
+            )
+            return bank
+
+        a_banks = [product(f"bank{t}", xa_words, xa_scales, t * P, wa_codes, wa_scales) for t in range(PACK)]
+
+        xb_scales = pick("xb_scales", U8, table_scales, two_sb, "wa_woven")
+        xb_words = pick("xb_words", U32, table_words, two_sb)
+
+        pairs = []
+        wb_woven = keep.tile([P, N, PACK], BF16, name="wb_woven", tag="wb_woven", align_bytes=64)
+        for t in range(PACK):
+            a_rows = keep.tile([P, H], F32, name=f"a_rows{t}", tag="wb_raw" if t == 2 else f"a_rows{t}")
+            nc.scalar.activation(a_rows[:], a_banks[t][:], COPY, scale=gt_abs[:, t : t + 1])
+            left = keep.tile([P, V], F32, name=f"left{t}")
+            nc.scalar.activation(left[:], a_rows[:].indirect(la_sb[:]), COPY)
+            right = keep.tile([P, V], F32, name=f"right{t}")
+            nc.scalar.activation(right[:], a_rows[:].indirect(lb_sb[:]), COPY)
+            pairs.append((left, right))
+            if t == 1:
+                weave(nc.scalar.copy, wb_woven, wb_raw, 0, N)
+
+        z_planes = keep.tile([P, PACK * H], F32, name="z_planes")
+        windows = [keep.tile([P, H], F32, name=f"placed{t}") for t in range(PACK - 1)] + [z_planes]
+        highs = {}
+        lows = {}
+
+        def order(t, op, dst):
+            name = f"high{t}" if dst is highs else f"low{t}"
+            dst[t] = keep.tile([P, V], F32, name=name, tag="wb_woven" if name == "high2" else name, align_bytes=64)
+            nc.vector.tensor_tensor(dst[t][:], pairs[t][0][:], pairs[t][1][:], op)
+
+        def place(t, offsets, src):
+            nc.vector.tensor_copy(windows[t][:].indirect(offsets[:]), src[t][:])
+
+        def join(t):
+            nc.scalar.copy(z_planes[:, (t + 1) * H : (t + 2) * H], windows[t][:])
+
+        wb_codes = keep.tile([P, N], U32, name="wb_codes", align_bytes=64)
+        wb_scales = keep.tile([P, N], U8, name="wb_scales", align_bytes=64)
+        z2_planes = keep.tile([P, PACK, N], BF16, name="z2_planes")
+        z2_woven = keep.tile([P, N, PACK], BF16, name="z2_woven", align_bytes=64)
+        z2_codes = keep.tile([P, N], U32, name="z2_codes", align_bytes=64)
+        z2_scales = keep.tile([P, N], U8, name="z2_scales", align_bytes=64)
+
+        order(0, ALU.max, highs)
+        order(0, ALU.min, lows)
+        place(0, la_sb, highs)
+        order(1, ALU.max, highs)
+        place(0, lb_sb, lows)
+        order(1, ALU.min, lows)
+        place(1, la_sb, highs)
+        quantize("wb", wb_woven, 0, N, wb_codes, wb_scales)
+        order(2, ALU.max, highs)
+        place(1, lb_sb, lows)
+        order(2, ALU.min, lows)
+        join(0)
+        for t in range(PACK):
+            bank = product(f"bank{PACK + t}", xb_words, xb_scales, t * P, wb_codes, wb_scales)
+            slot = (t + 1) % PACK
+            nc.scalar.activation(z2_planes[:, slot, :], bank[:], COPY, scale=gi_signed[:, t : t + 1])
+        join(1)
+        weave(nc.scalar.copy, z2_woven, z2_planes, 0, N // 2)
+        place(2, la_sb, highs)
+        order(3, ALU.max, highs)
+        place(2, lb_sb, lows)
+        order(3, ALU.min, lows)
+        join(2)
+        weave(nc.scalar.copy, z2_woven, z2_planes, N // 2, N)
+        place(3, la_sb, highs)
+        quantize("z2", z2_woven, 0, N, z2_codes, z2_scales)
+        place(3, lb_sb, lows)
+
+        z_view = z_planes[:].rearrange("p (t c) -> p t c", t=PACK)
+        z_woven = [keep.tile([P, P, PACK], BF16, name=f"z_woven{c}", align_bytes=64) for c in range(4)]
+        z_codes = [keep.tile([P, P], U32, name=f"z_codes{c}", align_bytes=64) for c in range(4)]
+        z_scales = [keep.tile([P, P], U8, name=f"z_scales{c}", align_bytes=64) for c in range(4)]
+
+        def weave_z(engine_copy, c):
+            weave(engine_copy, z_woven[c], z_view[:, :, c * P : (c + 1) * P], 0, P)
+
+        def finish(c, on_scalar):
+            quantize("z", z_woven[c], 0, P, z_codes[c], z_scales[c])
+            bank = product(f"bank{c}", z_codes[c], z_scales[c], 0, z2_codes, z2_scales)
+            result = keep.tile([P, N], F32, name=f"result{c}")
+            if on_scalar:
+                nc.scalar.activation(result[:], bank[:], COPY, scale=0.0625)
+            else:
+                nc.vector.tensor_scalar(result[:], bank[:], 0.0625, None, ALU.mult)
+            nc.sync.dma_start(out[c * P : (c + 1) * P, :], result[:])
+
+        weave_z(nc.scalar.copy, 3)
+        weave_z(nc.vector.tensor_copy, 0)
+        weave_z(nc.vector.tensor_copy, 1)
+        finish(0, True)
+        weave_z(nc.vector.tensor_copy, 2)
+        finish(1, True)
+        finish(3, False)
+        finish(2, True)

@@ -18,12 +18,21 @@ COPY = mybir.ActivationFunctionType.Copy
 P = 128
 PACK = 4
 LINE = 4
+LIST_COL = 16
+HALF = 256
+EARLY = 384
+LAST = PACK - 1
+OUT_SCALE = 0.0625
+
+XB_WORDS_AT, WA_LATE_AT = 0, 1024
+A1_AT, LOW0_AT, WB_WOVEN_AT = 4096, 4096, 5120
+WA_EARLY_AT, XA_WORDS_AT, GT_ABS_AT, GT_POS_AT = 9216, 9216, 11264, 11328
 
 
-def weave(engine_copy, woven, planes, first, last):
+def weave(engine_copy, woven, slots, first, last):
     engine_copy(
         out=woven[:, first:last, :].rearrange("p (c i) t -> p c t i", i=LINE),
-        in_=planes[:, :, first:last].rearrange("p t (c i) -> p c t i", i=LINE),
+        in_=slots[:, :, first:last].rearrange("p t (c i) -> p c t i", i=LINE),
     )
 
 
@@ -34,163 +43,231 @@ def tile_picked_momord_none_p_kernel(
 
     with ExitStack() as ctx:
         keep = ctx.enter_context(tc.tile_pool(name="keep", bufs=1))
+        placed = ctx.enter_context(tc.tile_pool(name="placed", bufs=1))
         psum = ctx.enter_context(tc.psum_pool(name="psum", bufs=1))
 
-        def quantize(name, woven, first, last, codes, scales):
+        def quantize(woven, codes, scales):
             nc.vector.quantize_mx(
-                out=codes[:, first:last].bitcast(FP8X4),
-                scales=scales[:, first:last],
-                in_=woven[:, first:last, :].rearrange("p c t -> p (c t)"),
+                out=codes.bitcast(FP8X4), scales=scales, in_=woven[:].rearrange("p c t -> p (c t)")
             )
 
-        table_scales = keep.tile([P, T], U8, name="table_scales")
-        nc.gpsimd.memset(table_scales[:].bitcast(I32), 0)
-        offs_sb = keep.tile([P, S // 16], U16, name="offs_sb")
-        nc.sync.dma_start(offs_sb[:], offs)
+        def multiply(acc, lhs_codes, lhs_scales, rhs_codes, rhs_scales):
+            nc.tensor.matmul_mx(
+                out=acc,
+                lhsT=lhs_codes.bitcast(FP8X4),
+                lhsT_scale=lhs_scales,
+                rhs=rhs_codes.bitcast(FP8X4),
+                rhs_scale=rhs_scales,
+                start=True,
+                stop=True,
+            )
+
+        def product(bank_name, lhs_codes, lhs_scales, rhs_codes, rhs_scales):
+            bank = psum.tile([P, rhs_codes.shape[1]], F32, name=bank_name, tag=bank_name)
+            multiply(bank[:], lhs_codes, lhs_scales, rhs_codes, rhs_scales)
+            return bank
+
+        scale_rows = keep.tile([P, T // 4], I32, name="scale_rows")
         for r in range(4):
-            nc.scalar.dma_start(table_scales[r:P:32, :].bitcast(I32), x_scales[0, r:16:4, :].bitcast(I32))
-        wa_raw = keep.tile([P, PACK, H], F32, name="wa_raw")
-        nc.sync.dma_start(wa_raw[:], wa.rearrange("(p j) c -> p j c", j=PACK))
+            queue = nc.sync if r < 2 else nc.scalar
+            queue.dma_start(scale_rows[r:P:32, :], x_scales[0, r:16:4, :].bitcast(I32))
+        offs_sb = keep.tile([P, S // LIST_COL], U16, name="offs_sb")
+        nc.sync.dma_start(offs_sb[:], offs)
+        two_sb = keep.tile([P, S // LIST_COL], U16, name="two_sb")
+        nc.sync.dma_start(two_sb[:], two)
+        wa_rows = wa.rearrange("(p j) c -> p j c", j=PACK)
+        wa_parts = (slice(0, EARLY), slice(EARLY, H))
+        wa_raw = [
+            keep.tile([P, PACK, width], F32, name=f"wa_raw{part}", tag=f"wa_raw{part}", align_bytes=64)
+            for part, width in enumerate((EARLY, H - EARLY))
+        ]
+        nc.sync.dma_start(wa_raw[0][:], wa_rows[:, :, wa_parts[0]])
         table_words = keep.tile([P, T], U32, name="table_words")
         nc.sync.dma_start(table_words[:].bitcast(I32), x_words[0].rearrange("p n r -> p (n r)").bitcast(I32))
         gt_sb = keep.tile([P, PACK], F32, name="gt_sb")
         nc.sync.dma_start(gt_sb[:], gt.rearrange("(p t) o -> p (t o)", t=PACK))
+        nc.sync.dma_start(wa_raw[1][:], wa_rows[:, :, wa_parts[1]])
+        la_sb = keep.tile([P, V // LIST_COL], U16, name="la_sb")
+        nc.sync.dma_start(la_sb[:], la)
+        lb_sb = keep.tile([P, V // LIST_COL], U16, name="lb_sb")
+        nc.sync.dma_start(lb_sb[:], lb)
+        wb_raw = keep.tile([P, PACK, N], F32, name="wb_raw")
+        nc.sync.dma_start(wb_raw[:], wb.rearrange("(p j) c -> p j c", j=PACK))
         gi_sb = keep.tile([P, PACK], F32, name="gi_sb")
         nc.sync.dma_start(gi_sb[:], gi.rearrange("(p t) o -> p (t o)", t=PACK))
-        two_sb = keep.tile([P, S // 16], U16, name="two_sb")
-        nc.sync.dma_start(two_sb[:], two)
-        la_sb = keep.tile([P, V // 16], U16, name="la_sb")
-        nc.sync.dma_start(la_sb[:], la)
-        lb_sb = keep.tile([P, V // 16], U16, name="lb_sb")
-        nc.sync.dma_start(lb_sb[:], lb)
-        wb_raw = keep.tile([P, PACK, N], F32, name="wb_raw", tag="wb_raw")
-        nc.sync.dma_start(wb_raw[:], wb.rearrange("(p j) c -> p j c", j=PACK))
 
-        def pick(name, dtype, table, offsets, tag=None):
-            picked = keep.tile([P, S], dtype, name=name, tag=tag or name, align_bytes=64)
+        table_scales = keep.tile([P, T], U8, name="table_scales")
+        nc.vector.memset(table_scales[:].bitcast(I32), 0)
+        for q in range(4):
+            live = slice(32 * q, 32 * q + 4)
+            nc.vector.tensor_copy(table_scales[live, :].bitcast(I32), scale_rows[live, :])
+
+        def pick(picked, table, offsets):
             nc.vector.tensor_copy(picked[:].rearrange("p (t m) -> p m t", t=PACK), table[:].indirect(offsets[:]))
-            return picked
 
-        xa_scales = pick("xa_scales", U8, table_scales, offs_sb)
-        wa_woven = keep.tile([P, H, PACK], BF16, name="wa_woven", tag="wa_woven", align_bytes=64)
-        weave(nc.scalar.copy, wa_woven, wa_raw, 0, 320)
-        weave(nc.vector.tensor_copy, wa_woven, wa_raw, 320, H)
-        gt_abs = keep.tile([P, PACK], F32, name="gt_abs")
-        nc.vector.scalar_tensor_tensor(gt_abs[:], gt_sb[:], -1.0, gt_sb[:], ALU.mult, ALU.max)
-        gt_pos = keep.tile([P, PACK], F32, name="gt_pos")
-        nc.vector.tensor_scalar(gt_pos[:], gt_sb[:], 0.0, 2.0, ALU.is_ge, ALU.mult)
+        xa_scales = keep.tile([P, S], U8, name="xa_scales", align_bytes=64)
+        pick(xa_scales, table_scales, offs_sb)
+        xb_scales = keep.tile([P, S], U8, name="xb_scales", align_bytes=64)
+        pick(xb_scales, table_scales, two_sb)
+
         wa_codes = keep.tile([P, H], U32, name="wa_codes", align_bytes=64)
         wa_scales = keep.tile([P, H], U8, name="wa_scales", align_bytes=64)
-        quantize("wa", wa_woven, 0, H, wa_codes, wa_scales)
-        gi_signed = keep.tile([P, PACK], F32, name="gi_signed")
-        nc.vector.scalar_tensor_tensor(gi_signed[:], gt_pos[:], -1.0, gi_sb[:], ALU.add, ALU.mult)
-        xa_words = pick("xa_words", U32, table_words, offs_sb)
+        wa_woven = [
+            placed.tile([P, EARLY, PACK], BF16, name="wa_woven0", align_bytes=64, offset=WA_EARLY_AT),
+            placed.tile([P, H - EARLY, PACK], BF16, name="wa_woven1", align_bytes=64, offset=WA_LATE_AT),
+        ]
 
-        def product(tag, words, scales, m0, codes, code_scales):
-            bank = psum.tile([P, 512], F32, name=tag, tag=tag)
-            nc.tensor.matmul_mx(
-                out=bank[:],
-                lhsT=words[:, m0 : m0 + P].bitcast(FP8X4),
-                lhsT_scale=scales[:, m0 : m0 + P],
-                rhs=codes[:].bitcast(FP8X4),
-                rhs_scale=code_scales[:],
-                start=True,
-                stop=True,
-            )
-            return bank
+        def prepare_wa(part):
+            weave(nc.scalar.copy, wa_woven[part], wa_raw[part], 0, wa_woven[part].shape[1])
+            quantize(wa_woven[part], wa_codes[:, wa_parts[part]], wa_scales[:, wa_parts[part]])
 
-        a_banks = [product(f"bank{t}", xa_words, xa_scales, t * P, wa_codes, wa_scales) for t in range(PACK)]
-
-        xb_scales = pick("xb_scales", U8, table_scales, two_sb, "wa_woven")
-        xb_words = pick("xb_words", U32, table_words, two_sb)
+        prepare_wa(0)
+        xa_words = placed.tile([P, S], U32, name="xa_words", align_bytes=64, offset=XA_WORDS_AT)
+        pick(xa_words, table_words, offs_sb)
+        gt_abs = placed.tile([P, PACK], F32, name="gt_abs", align_bytes=64, offset=GT_ABS_AT)
+        nc.vector.scalar_tensor_tensor(gt_abs[:], gt_sb[:], -1.0, gt_sb[:], ALU.mult, ALU.max)
+        gt_pos = placed.tile([P, PACK], F32, name="gt_pos", align_bytes=64, offset=GT_POS_AT)
+        nc.vector.tensor_scalar(gt_pos[:], gt_sb[:], 0.0, 2.0, ALU.is_ge, ALU.mult)
+        prepare_wa(1)
+        xb_words = placed.tile([P, S], U32, name="xb_words", align_bytes=64, offset=XB_WORDS_AT)
+        pick(xb_words, table_words, two_sb)
 
         pairs = []
-        wb_woven = keep.tile([P, N, PACK], BF16, name="wb_woven", tag="wb_woven", align_bytes=64)
         for t in range(PACK):
-            a_rows = keep.tile([P, H], F32, name=f"a_rows{t}", tag="wb_raw" if t == 2 else f"a_rows{t}")
-            nc.scalar.activation(a_rows[:], a_banks[t][:], COPY, scale=gt_abs[:, t : t + 1])
-            left = keep.tile([P, V], F32, name=f"left{t}")
-            nc.scalar.activation(left[:], a_rows[:].indirect(la_sb[:]), COPY)
-            right = keep.tile([P, V], F32, name=f"right{t}")
-            nc.scalar.activation(right[:], a_rows[:].indirect(lb_sb[:]), COPY)
-            pairs.append((left, right))
+            slot_cols = slice(t * P, (t + 1) * P)
             if t == 1:
+                a_rows = placed.tile([P, H], F32, name="a_rows1", align_bytes=64, offset=A1_AT)
+            else:
+                a_tag = "wa_raw1" if t == 0 else f"a_rows{t}"
+                a_rows = keep.tile([P, H], F32, name=f"a_rows{t}", tag=a_tag, align_bytes=64)
+            if t == 0:
+                banks = [("bank1", [0, HALF]), ("bank0", [HALF, EARLY, H])]
+            else:
+                banks = [("bank0", [0, H])]
+            for bank_name, cuts in banks:
+                first, last = cuts[0], cuts[-1]
+                a_bank = psum.tile([P, last - first], F32, name=bank_name, tag=bank_name)
+                for begin, end in zip(cuts, cuts[1:]):
+                    multiply(
+                        a_bank[:, begin - first : end - first],
+                        xa_words[:, slot_cols],
+                        xa_scales[:, slot_cols],
+                        wa_codes[:, begin:end],
+                        wa_scales[:, begin:end],
+                    )
+                nc.scalar.activation(a_rows[:, first:last], a_bank[:], COPY, scale=gt_abs[:, t : t + 1])
+            by_la = keep.tile([P, V], F32, name=f"by_la{t}")
+            nc.scalar.activation(by_la[:], a_rows[:].indirect(la_sb[:]), COPY)
+            by_lb = keep.tile([P, V], F32, name=f"by_lb{t}")
+            if t == 0:
+                nc.vector.tensor_copy(by_lb[:], a_rows[:].indirect(lb_sb[:]))
+            else:
+                nc.scalar.activation(by_lb[:], a_rows[:].indirect(lb_sb[:]), COPY)
+            pairs.append((by_la, by_lb))
+            if t == 1:
+                wb_woven = placed.tile([P, N, PACK], BF16, name="wb_woven", align_bytes=64, offset=WB_WOVEN_AT)
                 weave(nc.scalar.copy, wb_woven, wb_raw, 0, N)
 
-        z_planes = keep.tile([P, PACK * H], F32, name="z_planes")
-        windows = [keep.tile([P, H], F32, name=f"placed{t}") for t in range(PACK - 1)] + [z_planes]
+        z_slots = keep.tile([P, PACK * H], F32, name="z_slots", tag=f"a_rows{LAST}", align_bytes=64)
+        windows = [keep.tile([P, H], F32, name=f"window{t}") for t in range(LAST)] + [z_slots]
         highs = {}
         lows = {}
 
-        def order(t, op, dst):
-            name = f"high{t}" if dst is highs else f"low{t}"
-            dst[t] = keep.tile([P, V], F32, name=name, tag="wb_woven" if name == "high2" else name, align_bytes=64)
-            nc.vector.tensor_tensor(dst[t][:], pairs[t][0][:], pairs[t][1][:], op)
+        def larger(t):
+            highs[t] = keep.tile([P, V], F32, name=f"high{t}", tag=f"high{t}", align_bytes=64)
+            nc.vector.tensor_tensor(highs[t][:], pairs[t][0][:], pairs[t][1][:], ALU.max)
 
-        def place(t, offsets, src):
-            nc.vector.tensor_copy(windows[t][:].indirect(offsets[:]), src[t][:])
+        def smaller(t):
+            if t == 0:
+                lows[t] = placed.tile([P, V], F32, name="low0", align_bytes=64, offset=LOW0_AT)
+            else:
+                low_tag = {1: "a_rows2", LAST: "z2_slots0"}.get(t, f"low{t}")
+                lows[t] = keep.tile([P, V], F32, name=f"low{t}", tag=low_tag, align_bytes=64)
+            nc.vector.tensor_tensor(lows[t][:], pairs[t][0][:], pairs[t][1][:], ALU.min)
 
-        def join(t):
-            nc.scalar.copy(z_planes[:, (t + 1) * H : (t + 2) * H], windows[t][:])
+        def scatter(t, offsets, values):
+            nc.vector.tensor_copy(windows[t][:].indirect(offsets[:]), values[t][:])
+
+        def join(t, engine_copy):
+            engine_copy(z_slots[:, (t + 1) * H : (t + 2) * H], windows[t][:])
 
         wb_codes = keep.tile([P, N], U32, name="wb_codes", align_bytes=64)
         wb_scales = keep.tile([P, N], U8, name="wb_scales", align_bytes=64)
-        z2_planes = keep.tile([P, PACK, N], BF16, name="z2_planes")
-        z2_woven = keep.tile([P, N, PACK], BF16, name="z2_woven", align_bytes=64)
+        halves = [slice(h * HALF, (h + 1) * HALF) for h in range(2)]
+        z2_slots = [
+            keep.tile([P, PACK, HALF], BF16, name=f"z2_slots{h}", tag=f"z2_slots{h}", align_bytes=64)
+            for h in range(2)
+        ]
+        z2_woven = [keep.tile([P, HALF, PACK], BF16, name=f"z2_woven{h}", align_bytes=64) for h in range(2)]
         z2_codes = keep.tile([P, N], U32, name="z2_codes", align_bytes=64)
         z2_scales = keep.tile([P, N], U8, name="z2_scales", align_bytes=64)
 
-        order(0, ALU.max, highs)
-        order(0, ALU.min, lows)
-        place(0, la_sb, highs)
-        order(1, ALU.max, highs)
-        place(0, lb_sb, lows)
-        order(1, ALU.min, lows)
-        place(1, la_sb, highs)
-        quantize("wb", wb_woven, 0, N, wb_codes, wb_scales)
-        order(2, ALU.max, highs)
-        place(1, lb_sb, lows)
-        order(2, ALU.min, lows)
-        join(0)
-        for t in range(PACK):
-            bank = product(f"bank{PACK + t}", xb_words, xb_scales, t * P, wb_codes, wb_scales)
-            slot = (t + 1) % PACK
-            nc.scalar.activation(z2_planes[:, slot, :], bank[:], COPY, scale=gi_signed[:, t : t + 1])
-        join(1)
-        weave(nc.scalar.copy, z2_woven, z2_planes, 0, N // 2)
-        place(2, la_sb, highs)
-        order(3, ALU.max, highs)
-        place(2, lb_sb, lows)
-        order(3, ALU.min, lows)
-        join(2)
-        weave(nc.scalar.copy, z2_woven, z2_planes, N // 2, N)
-        place(3, la_sb, highs)
-        quantize("z2", z2_woven, 0, N, z2_codes, z2_scales)
-        place(3, lb_sb, lows)
+        def quantize_z2(h):
+            quantize(z2_woven[h], z2_codes[:, halves[h]], z2_scales[:, halves[h]])
 
-        z_view = z_planes[:].rearrange("p (t c) -> p t c", t=PACK)
-        z_woven = [keep.tile([P, P, PACK], BF16, name=f"z_woven{c}", align_bytes=64) for c in range(4)]
-        z_codes = [keep.tile([P, P], U32, name=f"z_codes{c}", align_bytes=64) for c in range(4)]
-        z_scales = [keep.tile([P, P], U8, name=f"z_scales{c}", align_bytes=64) for c in range(4)]
+        larger(0)
+        scatter(0, la_sb, highs)
+        larger(1)
+        smaller(0)
+        scatter(1, la_sb, highs)
+        scatter(0, lb_sb, lows)
+        gi_signed = keep.tile([P, PACK], F32, name="gi_signed", tag="high0", align_bytes=64)
+        nc.vector.scalar_tensor_tensor(gi_signed[:], gt_pos[:], -1.0, gi_sb[:], ALU.add, ALU.mult)
+        quantize(wb_woven, wb_codes[:], wb_scales[:])
+        larger(2)
+        smaller(1)
+        smaller(2)
+        scatter(2, la_sb, highs)
+        scatter(1, lb_sb, lows)
+        scatter(2, lb_sb, lows)
+        larger(LAST)
+
+        for t in range(PACK):
+            slot_cols = slice(t * P, (t + 1) * P)
+            b_bank = product(
+                f"bank{PACK + t}", xb_words[:, slot_cols], xb_scales[:, slot_cols], wb_codes[:], wb_scales[:]
+            )
+            for h in range(2):
+                nc.scalar.activation(
+                    z2_slots[h][:, (t + 1) % PACK, :], b_bank[:, halves[h]], COPY, scale=gi_signed[:, t : t + 1]
+                )
+
+        join(2, nc.vector.tensor_copy)
+        join(0, nc.scalar.copy)
+        join(1, nc.scalar.copy)
+        for h in range(2):
+            weave(nc.scalar.copy, z2_woven[h], z2_slots[h], 0, HALF)
+        scatter(LAST, la_sb, highs)
+        smaller(LAST)
+        quantize_z2(0)
+        scatter(LAST, lb_sb, lows)
+
+        blocks = H // P
+        z_view = z_slots[:].rearrange("p (t c) -> p t c", t=PACK)
+        z_woven = [keep.tile([P, P, PACK], BF16, name=f"z_woven{c}", align_bytes=64) for c in range(blocks)]
+        z_codes = [keep.tile([P, P], U32, name=f"z_codes{c}", align_bytes=64) for c in range(blocks)]
+        z_scales = [keep.tile([P, P], U8, name=f"z_scales{c}", align_bytes=64) for c in range(blocks)]
 
         def weave_z(engine_copy, c):
             weave(engine_copy, z_woven[c], z_view[:, :, c * P : (c + 1) * P], 0, P)
 
-        def finish(c, on_scalar):
-            quantize("z", z_woven[c], 0, P, z_codes[c], z_scales[c])
-            bank = product(f"bank{c}", z_codes[c], z_scales[c], 0, z2_codes, z2_scales)
-            result = keep.tile([P, N], F32, name=f"result{c}")
-            if on_scalar:
-                nc.scalar.activation(result[:], bank[:], COPY, scale=0.0625)
-            else:
-                nc.vector.tensor_scalar(result[:], bank[:], 0.0625, None, ALU.mult)
-            nc.sync.dma_start(out[c * P : (c + 1) * P, :], result[:])
-
-        weave_z(nc.scalar.copy, 3)
         weave_z(nc.vector.tensor_copy, 0)
+        weave_z(nc.scalar.copy, 2)
         weave_z(nc.vector.tensor_copy, 1)
-        finish(0, True)
-        weave_z(nc.vector.tensor_copy, 2)
-        finish(1, True)
-        finish(3, False)
-        finish(2, True)
+        weave_z(nc.scalar.copy, 3)
+        for c in range(blocks):
+            quantize(z_woven[c], z_codes[c][:], z_scales[c][:])
+            if c == 0:
+                quantize_z2(1)
+
+        for c in range(blocks):
+            for h in range(2):
+                cv_bank = product(
+                    f"bank{2 * c + h}", z_codes[c][:], z_scales[c][:], z2_codes[:, halves[h]], z2_scales[:, halves[h]]
+                )
+                result = keep.tile([P, HALF], F32, name=f"result{c}_{h}")
+                if h == 0:
+                    nc.scalar.activation(result[:], cv_bank[:], COPY, scale=OUT_SCALE)
+                else:
+                    nc.vector.tensor_scalar(result[:], cv_bank[:], OUT_SCALE, None, ALU.mult)
+                nc.sync.dma_start(out[c * P : (c + 1) * P, halves[h]], result[:])

from contextlib import ExitStack

import concourse.mybir as mybir

K, T, S, V, N, H = 512, 2048, 512, 256, 512, 512
FLOPS = 2 * S * K * H + 2 * S * K * N + 2 * S * H * N

F32 = mybir.dt.float32
BF16 = mybir.dt.bfloat16
I32 = mybir.dt.int32
U32 = mybir.dt.uint32
U16 = mybir.dt.uint16
U8 = mybir.dt.uint8
FP8X4 = mybir.dt.float8_e4m3fn_x4
ALU = mybir.AluOpType
COPY = mybir.ActivationFunctionType.Copy

P = 128
PACK = 4
LINE = 4
LIST_COL = 16
HALF = 256
EARLY = 384
LAST = PACK - 1
OUT_SCALE = 0.0625

XB_WORDS_AT, WA_LATE_AT = 0, 1024
A1_AT, LOW0_AT, WB_WOVEN_AT = 4096, 4096, 5120
WA_EARLY_AT, XA_WORDS_AT, GT_ABS_AT, GT_POS_AT = 9216, 9216, 11264, 11328


def weave(engine_copy, woven, slots, first, last):
    engine_copy(
        out=woven[:, first:last, :].rearrange("p (c i) t -> p c t i", i=LINE),
        in_=slots[:, :, first:last].rearrange("p t (c i) -> p c t i", i=LINE),
    )


def tile_picked_momord_none_p_kernel(
    tc, x_words, x_scales, wa, wb, gt, gi, offs, two, la, lb, out
):
    nc = tc.nc

    with ExitStack() as ctx:
        keep = ctx.enter_context(tc.tile_pool(name="keep", bufs=1))
        placed = ctx.enter_context(tc.tile_pool(name="placed", bufs=1))
        psum = ctx.enter_context(tc.psum_pool(name="psum", bufs=1))

        def quantize(woven, codes, scales):
            nc.vector.quantize_mx(
                out=codes.bitcast(FP8X4), scales=scales, in_=woven[:].rearrange("p c t -> p (c t)")
            )

        def multiply(acc, lhs_codes, lhs_scales, rhs_codes, rhs_scales):
            nc.tensor.matmul_mx(
                out=acc,
                lhsT=lhs_codes.bitcast(FP8X4),
                lhsT_scale=lhs_scales,
                rhs=rhs_codes.bitcast(FP8X4),
                rhs_scale=rhs_scales,
                start=True,
                stop=True,
            )

        def product(bank_name, lhs_codes, lhs_scales, rhs_codes, rhs_scales):
            bank = psum.tile([P, rhs_codes.shape[1]], F32, name=bank_name, tag=bank_name)
            multiply(bank[:], lhs_codes, lhs_scales, rhs_codes, rhs_scales)
            return bank

        scale_rows = keep.tile([P, T // 4], I32, name="scale_rows")
        for r in range(4):
            queue = nc.sync if r < 2 else nc.scalar
            queue.dma_start(scale_rows[r:P:32, :], x_scales[0, r:16:4, :].bitcast(I32))
        offs_sb = keep.tile([P, S // LIST_COL], U16, name="offs_sb")
        nc.sync.dma_start(offs_sb[:], offs)
        two_sb = keep.tile([P, S // LIST_COL], U16, name="two_sb")
        nc.sync.dma_start(two_sb[:], two)
        wa_rows = wa.rearrange("(p j) c -> p j c", j=PACK)
        wa_parts = (slice(0, EARLY), slice(EARLY, H))
        wa_raw = [
            keep.tile([P, PACK, width], F32, name=f"wa_raw{part}", tag=f"wa_raw{part}", align_bytes=64)
            for part, width in enumerate((EARLY, H - EARLY))
        ]
        nc.sync.dma_start(wa_raw[0][:], wa_rows[:, :, wa_parts[0]])
        table_words = keep.tile([P, T], U32, name="table_words")
        nc.sync.dma_start(table_words[:].bitcast(I32), x_words[0].rearrange("p n r -> p (n r)").bitcast(I32))
        gt_sb = keep.tile([P, PACK], F32, name="gt_sb")
        nc.sync.dma_start(gt_sb[:], gt.rearrange("(p t) o -> p (t o)", t=PACK))
        nc.sync.dma_start(wa_raw[1][:], wa_rows[:, :, wa_parts[1]])
        la_sb = keep.tile([P, V // LIST_COL], U16, name="la_sb")
        nc.sync.dma_start(la_sb[:], la)
        lb_sb = keep.tile([P, V // LIST_COL], U16, name="lb_sb")
        nc.sync.dma_start(lb_sb[:], lb)
        wb_raw = keep.tile([P, PACK, N], F32, name="wb_raw")
        nc.sync.dma_start(wb_raw[:], wb.rearrange("(p j) c -> p j c", j=PACK))
        gi_sb = keep.tile([P, PACK], F32, name="gi_sb")
        nc.sync.dma_start(gi_sb[:], gi.rearrange("(p t) o -> p (t o)", t=PACK))

        table_scales = keep.tile([P, T], U8, name="table_scales")
        nc.vector.memset(table_scales[:].bitcast(I32), 0)
        for q in range(4):
            live = slice(32 * q, 32 * q + 4)
            nc.vector.tensor_copy(table_scales[live, :].bitcast(I32), scale_rows[live, :])

        def pick(picked, table, offsets):
            nc.vector.tensor_copy(picked[:].rearrange("p (t m) -> p m t", t=PACK), table[:].indirect(offsets[:]))

        xa_scales = keep.tile([P, S], U8, name="xa_scales", align_bytes=64)
        pick(xa_scales, table_scales, offs_sb)
        xb_scales = keep.tile([P, S], U8, name="xb_scales", align_bytes=64)
        pick(xb_scales, table_scales, two_sb)

        wa_codes = keep.tile([P, H], U32, name="wa_codes", align_bytes=64)
        wa_scales = keep.tile([P, H], U8, name="wa_scales", align_bytes=64)
        wa_woven = [
            placed.tile([P, EARLY, PACK], BF16, name="wa_woven0", align_bytes=64, offset=WA_EARLY_AT),
            placed.tile([P, H - EARLY, PACK], BF16, name="wa_woven1", align_bytes=64, offset=WA_LATE_AT),
        ]

        def prepare_wa(part):
            weave(nc.scalar.copy, wa_woven[part], wa_raw[part], 0, wa_woven[part].shape[1])
            quantize(wa_woven[part], wa_codes[:, wa_parts[part]], wa_scales[:, wa_parts[part]])

        prepare_wa(0)
        xa_words = placed.tile([P, S], U32, name="xa_words", align_bytes=64, offset=XA_WORDS_AT)
        pick(xa_words, table_words, offs_sb)
        gt_abs = placed.tile([P, PACK], F32, name="gt_abs", align_bytes=64, offset=GT_ABS_AT)
        nc.vector.scalar_tensor_tensor(gt_abs[:], gt_sb[:], -1.0, gt_sb[:], ALU.mult, ALU.max)
        gt_pos = placed.tile([P, PACK], F32, name="gt_pos", align_bytes=64, offset=GT_POS_AT)
        nc.vector.tensor_scalar(gt_pos[:], gt_sb[:], 0.0, 2.0, ALU.is_ge, ALU.mult)
        prepare_wa(1)
        xb_words = placed.tile([P, S], U32, name="xb_words", align_bytes=64, offset=XB_WORDS_AT)
        pick(xb_words, table_words, two_sb)

        pairs = []
        for t in range(PACK):
            slot_cols = slice(t * P, (t + 1) * P)
            if t == 1:
                a_rows = placed.tile([P, H], F32, name="a_rows1", align_bytes=64, offset=A1_AT)
            else:
                a_tag = "wa_raw1" if t == 0 else f"a_rows{t}"
                a_rows = keep.tile([P, H], F32, name=f"a_rows{t}", tag=a_tag, align_bytes=64)
            if t == 0:
                banks = [("bank1", [0, HALF]), ("bank0", [HALF, EARLY, H])]
            else:
                banks = [("bank0", [0, H])]
            for bank_name, cuts in banks:
                first, last = cuts[0], cuts[-1]
                a_bank = psum.tile([P, last - first], F32, name=bank_name, tag=bank_name)
                for begin, end in zip(cuts, cuts[1:]):
                    multiply(
                        a_bank[:, begin - first : end - first],
                        xa_words[:, slot_cols],
                        xa_scales[:, slot_cols],
                        wa_codes[:, begin:end],
                        wa_scales[:, begin:end],
                    )
                nc.scalar.activation(a_rows[:, first:last], a_bank[:], COPY, scale=gt_abs[:, t : t + 1])
            by_la = keep.tile([P, V], F32, name=f"by_la{t}")
            nc.scalar.activation(by_la[:], a_rows[:].indirect(la_sb[:]), COPY)
            by_lb = keep.tile([P, V], F32, name=f"by_lb{t}")
            if t == 0:
                nc.vector.tensor_copy(by_lb[:], a_rows[:].indirect(lb_sb[:]))
            else:
                nc.scalar.activation(by_lb[:], a_rows[:].indirect(lb_sb[:]), COPY)
            pairs.append((by_la, by_lb))
            if t == 1:
                wb_woven = placed.tile([P, N, PACK], BF16, name="wb_woven", align_bytes=64, offset=WB_WOVEN_AT)
                weave(nc.scalar.copy, wb_woven, wb_raw, 0, N)

        z_slots = keep.tile([P, PACK * H], F32, name="z_slots", tag=f"a_rows{LAST}", align_bytes=64)
        windows = [keep.tile([P, H], F32, name=f"window{t}") for t in range(LAST)] + [z_slots]
        highs = {}
        lows = {}

        def larger(t):
            highs[t] = keep.tile([P, V], F32, name=f"high{t}", tag=f"high{t}", align_bytes=64)
            nc.vector.tensor_tensor(highs[t][:], pairs[t][0][:], pairs[t][1][:], ALU.max)

        def smaller(t):
            if t == 0:
                lows[t] = placed.tile([P, V], F32, name="low0", align_bytes=64, offset=LOW0_AT)
            else:
                low_tag = {1: "a_rows2", LAST: "z2_slots0"}.get(t, f"low{t}")
                lows[t] = keep.tile([P, V], F32, name=f"low{t}", tag=low_tag, align_bytes=64)
            nc.vector.tensor_tensor(lows[t][:], pairs[t][0][:], pairs[t][1][:], ALU.min)

        def scatter(t, offsets, values):
            nc.vector.tensor_copy(windows[t][:].indirect(offsets[:]), values[t][:])

        def join(t, engine_copy):
            engine_copy(z_slots[:, (t + 1) * H : (t + 2) * H], windows[t][:])

        wb_codes = keep.tile([P, N], U32, name="wb_codes", align_bytes=64)
        wb_scales = keep.tile([P, N], U8, name="wb_scales", align_bytes=64)
        halves = [slice(h * HALF, (h + 1) * HALF) for h in range(2)]
        z2_slots = [
            keep.tile([P, PACK, HALF], BF16, name=f"z2_slots{h}", tag=f"z2_slots{h}", align_bytes=64)
            for h in range(2)
        ]
        z2_woven = [keep.tile([P, HALF, PACK], BF16, name=f"z2_woven{h}", align_bytes=64) for h in range(2)]
        z2_codes = keep.tile([P, N], U32, name="z2_codes", align_bytes=64)
        z2_scales = keep.tile([P, N], U8, name="z2_scales", align_bytes=64)

        def quantize_z2(h):
            quantize(z2_woven[h], z2_codes[:, halves[h]], z2_scales[:, halves[h]])

        larger(0)
        scatter(0, la_sb, highs)
        larger(1)
        smaller(0)
        scatter(1, la_sb, highs)
        scatter(0, lb_sb, lows)
        gi_signed = keep.tile([P, PACK], F32, name="gi_signed", tag="high0", align_bytes=64)
        nc.vector.scalar_tensor_tensor(gi_signed[:], gt_pos[:], -1.0, gi_sb[:], ALU.add, ALU.mult)
        quantize(wb_woven, wb_codes[:], wb_scales[:])
        larger(2)
        smaller(1)
        smaller(2)
        scatter(2, la_sb, highs)
        scatter(1, lb_sb, lows)
        scatter(2, lb_sb, lows)
        larger(LAST)

        for t in range(PACK):
            slot_cols = slice(t * P, (t + 1) * P)
            b_bank = product(
                f"bank{PACK + t}", xb_words[:, slot_cols], xb_scales[:, slot_cols], wb_codes[:], wb_scales[:]
            )
            for h in range(2):
                nc.scalar.activation(
                    z2_slots[h][:, (t + 1) % PACK, :], b_bank[:, halves[h]], COPY, scale=gi_signed[:, t : t + 1]
                )

        join(2, nc.vector.tensor_copy)
        join(0, nc.scalar.copy)
        join(1, nc.scalar.copy)
        for h in range(2):
            weave(nc.scalar.copy, z2_woven[h], z2_slots[h], 0, HALF)
        scatter(LAST, la_sb, highs)
        smaller(LAST)
        quantize_z2(0)
        scatter(LAST, lb_sb, lows)

        blocks = H // P
        z_view = z_slots[:].rearrange("p (t c) -> p t c", t=PACK)
        z_woven = [keep.tile([P, P, PACK], BF16, name=f"z_woven{c}", align_bytes=64) for c in range(blocks)]
        z_codes = [keep.tile([P, P], U32, name=f"z_codes{c}", align_bytes=64) for c in range(blocks)]
        z_scales = [keep.tile([P, P], U8, name=f"z_scales{c}", align_bytes=64) for c in range(blocks)]

        def weave_z(engine_copy, c):
            weave(engine_copy, z_woven[c], z_view[:, :, c * P : (c + 1) * P], 0, P)

        weave_z(nc.vector.tensor_copy, 0)
        weave_z(nc.scalar.copy, 2)
        weave_z(nc.vector.tensor_copy, 1)
        weave_z(nc.scalar.copy, 3)
        for c in range(blocks):
            quantize(z_woven[c], z_codes[c][:], z_scales[c][:])
            if c == 0:
                quantize_z2(1)

        for c in range(blocks):
            for h in range(2):
                cv_bank = product(
                    f"bank{2 * c + h}", z_codes[c][:], z_scales[c][:], z2_codes[:, halves[h]], z2_scales[:, halves[h]]
                )
                result = keep.tile([P, HALF], F32, name=f"result{c}_{h}")
                if h == 0:
                    nc.scalar.activation(result[:], cv_bank[:], COPY, scale=OUT_SCALE)
                else:
                    nc.vector.tensor_scalar(result[:], cv_bank[:], OUT_SCALE, None, ALU.mult)
                nc.sync.dma_start(out[c * P : (c + 1) * P, halves[h]], result[:])
